import numpy as np
import ml_dtypes


def mxq(x, axis, fmt="e4m3"):
    dtype, down = {"e4m3": (ml_dtypes.float8_e4m3fn, 7), "e5m2": (ml_dtypes.float8_e5m2, 14)}[fmt]
    v = np.moveaxis(np.asarray(x, np.float32).astype(ml_dtypes.bfloat16).astype(np.float64), axis, -1)
    blocks = v.reshape(v.shape[:-1] + (-1, 32))
    amax = np.abs(blocks).max(-1, keepdims=True)
    byte = np.maximum(np.where(amax > 0, np.frexp(amax)[1] - 1 + 127, 0) - down, 1)
    scale = np.exp2(byte - 127.0)
    codes = (blocks / scale).astype(np.float32).astype(dtype).astype(np.float64)
    return np.moveaxis((codes * scale).reshape(v.shape), -1, axis)


WIDE = False


def mx_kscale(k):
    if not WIDE:
        return np.ones(k)
    levels = np.array([10, -10, 5, -5, 0])
    if k % 512:
        return np.exp2(np.random.permutation(np.resize(levels, k // 32))).repeat(32)
    a = np.empty((k // 512, 16))
    for p in range(k // 512):
        a[p, :8] = np.random.permutation(np.resize(levels, 8))
        for g in range(8):
            far = levels[np.abs(levels - a[p, g]) >= 10]
            a[p, g + 8] = far[np.random.randint(len(far))]
    return np.exp2(a.ravel()).repeat(32)


def f64(x):
    return np.asarray(x).astype(np.float64)


def striped(idx):
    return np.tile(idx.reshape(-1, 16).T, (8, 1)).astype(np.uint16)


def unstriped(offs):
    return offs[:16].T.reshape(-1).astype(np.int64)


def striped8(idx):
    return np.concatenate([x.reshape(-1, 16).T for x in idx]).astype(np.uint16)


def runs(offs, k):
    lists = np.stack([offs[16 * r : 16 * r + 16].T.reshape(-1) for r in range(8)]).astype(np.int64)
    return lists[np.arange(k) % 512 // 64]


def pack_weight(w):
    k, n = w.shape
    w = f64(np.asarray(w, np.float32).astype(ml_dtypes.bfloat16)).reshape(k // 32, 32, n)
    amax = np.abs(w).max(1)
    byte = np.clip(np.where(amax > 0, np.frexp(amax)[1] - 1 + 127 - 7, 1), 1, 254)
    scaled = (w * np.exp2(127.0 - byte)[:, None, :]).reshape(k, n).astype(np.float32)
    words = np.ascontiguousarray(scaled.reshape(k // 512, 128, 4, n).transpose(0, 1, 3, 2)).astype(ml_dtypes.float8_e4m3fn).view(np.uint8)
    return words, np.ascontiguousarray(byte.astype(np.uint8).reshape(k // 512, 16, n))


def unpack_weight(words, scales):
    g, p, n, _ = words.shape
    vals = np.ascontiguousarray(words).view(ml_dtypes.float8_e4m3fn).astype(np.float64) * np.repeat(np.exp2(scales.astype(np.float64) - 127.0), 8, axis=1)[..., None]
    return vals.transpose(0, 1, 3, 2).reshape(g * 512, n)


K, T, S, V, G, H, C = 512, 2048, 1024, 512, 2048, 512, 512


def setup_inputs():
    n = np.random.standard_normal
    s = mx_kscale(K)[:, None]
    packed_xT = pack_weight(n((K, T)) * s)
    packed_dT = pack_weight(n((K, G)) / s)
    return {
        "x_words": packed_xT[0],
        "x_scales": packed_xT[1],
        "d_words": packed_dT[0],
        "d_scales": packed_dT[1],
        "gs": (np.random.uniform(0.5, 1.5, (K, 1)) / s).astype(np.float32),
        "offs": striped(np.random.permutation(T)[:S]),
        "k1": striped8(np.random.randint(0, G, (8, H))),
        "n1": striped8(np.stack([np.random.permutation(S) for _ in range(8)])),
        "cand": striped(np.random.permutation(T)[:C]),
        "n2": striped8(np.stack([np.random.permutation(V) for _ in range(8)])),
    }


def reference(x_words, x_scales, d_words, d_scales, gs, offs, k1, n1, cand, n2):
    x_cand = unpack_weight(x_words, x_scales)[:, unstriped(cand)]
    d_k1 = unpack_weight(d_words, d_scales)[np.arange(K)[:, None], runs(k1, K)]
    xq = unpack_weight(x_words, x_scales)[:, unstriped(offs)]
    h = 0.0625 * (d_k1.T @ xq)
    ln = h[np.arange(H)[:, None], runs(n1, H)]
    sq = (ln) ** 2
    ms = sq.reshape(H, V, 2).sum(axis=2)
    z = f64(gs) * np.sqrt(ms + 0.1)
    s = 0.0625 * ((x_cand.T @ mxq(z, 0, "e4m3")))
    return s - (s[np.arange(C)[:, None], runs(n2, C)])

@@ -1,0 +1,180 @@
+from contextlib import ExitStack
+
+import concourse.mybir as mybir
+
+K, T, S, V, G, H, C = 512, 2048, 1024, 512, 2048, 512, 512
+FLOPS = 2 * K * H * S + 2 * K * C * V
+
+F32 = mybir.dt.float32
+BF16 = mybir.dt.bfloat16
+I32 = mybir.dt.int32
+U32 = mybir.dt.uint32
+U16 = mybir.dt.uint16
+U8 = mybir.dt.uint8
+FP8X4 = mybir.dt.float8_e4m3fn_x4
+ACT = mybir.ActivationFunctionType
+ALU = mybir.AluOpType
+
+P = 128
+PACK = 4
+LANES = 16
+BANK = 512
+CHUNKS = ((0, 256), (256, 128), (384, 128))
+
+
+def tile_picked_pqcprmsdif_none_p_kernel(
+    tc, x_words, x_scales, d_words, d_scales, gs, offs, k1, n1, cand, n2, out
+):
+    nc = tc.nc
+    with ExitStack() as ctx:
+        lists = ctx.enter_context(tc.tile_pool(name="lists", bufs=1))
+        keep = ctx.enter_context(tc.tile_pool(name="keep", bufs=1))
+        ring = ctx.enter_context(tc.tile_pool(name="ring", bufs=2))
+        psum = ctx.enter_context(tc.psum_pool(name="psum", bufs=1))
+
+        k1_sb = lists.tile([P, H // LANES], U16, name="k1_sb")
+        offs_sb = lists.tile([P, S // LANES], U16, name="offs_sb")
+        cand_sb = lists.tile([P, C // LANES], U16, name="cand_sb")
+        n1_sb = lists.tile([P, S // LANES], U16, name="n1_sb")
+        n2_sb = lists.tile([P, V // LANES], U16, name="n2_sb")
+
+        d_byte_table = keep.tile([P, G], U8, name="d_byte_table", align_bytes=64)
+        x_byte_table = keep.tile([P, T], U8, name="x_byte_table", align_bytes=64)
+        d_word_table = keep.tile([P, G], U32, name="d_word_table", align_bytes=64)
+        x_word_table = keep.tile([P, T], U32, name="x_word_table", align_bytes=64)
+        d_plane = keep.tile([P, H], U8, name="d_plane", align_bytes=64)
+        gs_sb = keep.tile([P, PACK], F32, name="gs_sb")
+
+        nc.gpsimd.memset(d_byte_table[:].bitcast(I32), 0)
+        nc.vector.memset(x_byte_table[:].bitcast(I32), 0)
+        nc.gpsimd.memset(d_plane[:].bitcast(I32), 0)
+
+        d_words_rows = d_words[0].rearrange("p c r -> p (c r)").bitcast(I32)
+        nc.sync.dma_start(k1_sb[:], k1)
+        nc.sync.dma_start(d_word_table[:, 0:BANK].bitcast(I32), d_words_rows[:, 0:BANK])
+        nc.sync.dma_start(d_byte_table[0:P:8, :].bitcast(I32), d_scales[0].bitcast(I32))
+        nc.sync.dma_start(offs_sb[:], offs)
+        for q in range(4):
+            nc.sync.dma_start(
+                x_byte_table[32 * q : 32 * q + 4, :].bitcast(I32), x_scales[0, 4 * q : 4 * q + 4, :].bitcast(I32)
+            )
+        nc.sync.dma_start(d_word_table[:, BANK:G].bitcast(I32), d_words_rows[:, BANK:G])
+        nc.sync.dma_start(x_word_table[:].bitcast(I32), x_words[0].rearrange("p c r -> p (c r)").bitcast(I32))
+        nc.sync.dma_start(n1_sb[:], n1)
+        nc.sync.dma_start(n2_sb[:], n2)
+        nc.sync.dma_start(cand_sb[:], cand)
+        nc.gpsimd.dma_start(gs_sb[:], gs.rearrange("(p t) o -> p (t o)", t=PACK))
+
+        warm = keep.tile([P, 1], F32, name="warm")
+        warm_in = keep.tile([P, 1], F32, name="warm_in")
+        nc.gpsimd.memset(warm_in[:], 1.0)
+        nc.scalar.activation(warm[:], warm_in[:], ACT.Sqrt)
+
+        d_bytes = keep.tile([P, H], U8, name="d_bytes", align_bytes=64)
+        nc.vector.tensor_copy(d_bytes[:], d_byte_table[:].indirect(k1_sb[:]))
+        d_bytes_dealt = keep.tile([P, PACK, P], U8, name="d_bytes_dealt", align_bytes=64)
+        nc.vector.tensor_copy(d_bytes_dealt[:], d_bytes[:].rearrange("p (m t) -> p t m", t=PACK))
+        dealt_rows = d_bytes_dealt[:].rearrange("p t m -> p (t m)")
+        for c in range(4):
+            nc.scalar.dma_start(d_plane[c:P:32, :].bitcast(I32), dealt_rows[8 * c : P : 32, :].bitcast(I32))
+
+        xq_bytes = keep.tile([P, S], U8, name="xq_bytes", align_bytes=64)
+        nc.vector.tensor_copy(xq_bytes[:], x_byte_table[:].indirect(offs_sb[:]))
+
+        d_picked = keep.tile([P, H], U32, name="d_picked", align_bytes=64)
+        nc.vector.tensor_copy(d_picked[:], d_word_table[:].indirect(k1_sb[:]))
+        d_codes = keep.tile([P, PACK, P], U32, name="d_codes", align_bytes=64)
+        nc.vector.tensor_copy(d_codes[:].bitcast(I32), d_picked[:].bitcast(I32).rearrange("p (m t) -> p t m", t=PACK))
+
+        xq_words = [keep.tile([P, BANK], U32, name=f"xq_words{u}", align_bytes=64) for u in range(2)]
+        for u in range(2):
+            nc.vector.tensor_copy(xq_words[u][:], x_word_table[:].indirect(offs_sb[:, 32 * u : 32 * (u + 1)]))
+
+        sq = [keep.tile([P, S], F32, name=f"sq{t}") for t in range(PACK)]
+
+        def first_product(t, u):
+            bank = psum.tile([P, BANK], F32, name=f"h_bank{t}{u}", tag=f"bank{2 * t + u}")
+            nc.tensor.matmul_mx(
+                out=bank[:],
+                lhsT=d_codes[:, t, :].bitcast(FP8X4),
+                lhsT_scale=d_plane[:, t * P : (t + 1) * P],
+                rhs=xq_words[u][:].bitcast(FP8X4),
+                rhs_scale=xq_bytes[:, u * BANK : (u + 1) * BANK],
+                start=True,
+                stop=True,
+            )
+            nc.scalar.activation(sq[t][:, u * BANK : (u + 1) * BANK], bank[:], ACT.Square, scale=0.0625)
+
+        for t, u in ((0, 0), (1, 0), (0, 1), (1, 1), (2, 0), (2, 1), (3, 0), (3, 1)):
+            first_product(t, u)
+
+        cand_bytes = keep.tile([P, C], U8, name="cand_bytes", align_bytes=64)
+        nc.vector.tensor_copy(cand_bytes[:], x_byte_table[:].indirect(cand_sb[:]))
+        cand_plane = keep.tile([P, PACK, P], U8, name="cand_plane", align_bytes=64)
+        nc.vector.tensor_copy(cand_plane[:], cand_bytes[:].rearrange("p (m t) -> p t m", t=PACK))
+        s_banks = [psum.tile([P, V], F32, name=f"s_bank{t}", tag=f"bank{t}") for t in range(PACK)]
+        quantised = []
+        for n, (v0, width) in enumerate(CHUNKS):
+            planes = keep.tile([P, PACK, width], BF16, name=f"planes{n}", align_bytes=64)
+            for t in range(PACK):
+                lined = ring.tile([P, width, 2], F32, name=f"lined{n}{t}", tag="lined", align_bytes=64)
+                nc.vector.tensor_copy(
+                    lined[:].rearrange("p v e -> p (v e)"),
+                    sq[t][:].indirect(n1_sb[:, 2 * v0 // LANES : 2 * (v0 + width) // LANES]),
+                )
+                ms = ring.tile([P, width], F32, name=f"ms{n}{t}", tag="ms", bufs=3)
+                nc.vector.tensor_tensor(ms[:], lined[:, :, 0], lined[:, :, 1], ALU.add)
+                root = keep.tile([P, width], F32, name=f"root{n}{t}")
+                nc.scalar.activation(root[:], ms[:], ACT.Sqrt, bias=0.1)
+                nc.scalar.activation(planes[:, t, :], root[:], ACT.Copy, scale=gs_sb[:, t : t + 1])
+            if n == len(CHUNKS) - 1:
+                cand_picked = ring.tile([P, C], U32, name="cand_picked", tag="lined", align_bytes=64)
+                nc.vector.tensor_copy(cand_picked[:], x_word_table[:].indirect(cand_sb[:]))
+                cand_codes = keep.tile([P, PACK, P], U32, name="cand_codes", align_bytes=64)
+                nc.vector.tensor_copy(
+                    cand_codes[:].bitcast(I32), cand_picked[:].bitcast(I32).rearrange("p (m t) -> p t m", t=PACK)
+                )
+            z = keep.tile([P, width, PACK], BF16, name=f"z{n}", align_bytes=64)
+            nc.scalar.copy(
+                z[:].rearrange("p (c i) t -> p c t i", i=4), planes[:].rearrange("p t (c i) -> p c t i", i=4)
+            )
+            z_codes = keep.tile([P, width], U32, name=f"z_codes{n}", align_bytes=64)
+            z_plane = keep.tile([P, width], U8, name=f"z_plane{n}", align_bytes=64)
+            nc.vector.quantize_mx(
+                out=z_codes[:].bitcast(FP8X4), scales=z_plane[:], in_=z[:].rearrange("p v t -> p (v t)")
+            )
+            quantised.append((z_codes, z_plane))
+
+        def second_product(t, n):
+            v0, width = CHUNKS[n]
+            z_codes, z_plane = quantised[n]
+            nc.tensor.matmul_mx(
+                out=s_banks[t][:, v0 : v0 + width],
+                lhsT=cand_codes[:, t, :].bitcast(FP8X4),
+                lhsT_scale=cand_plane[:, t, :],
+                rhs=z_codes[:].bitcast(FP8X4),
+                rhs_scale=z_plane[:],
+                start=True,
+                stop=True,
+            )
+
+        for t in range(PACK):
+            for n in range(len(CHUNKS)):
+                second_product(t, n)
+
+        out_rows = out.rearrange("(p t) v -> p t v", t=PACK)
+        for t in range(PACK):
+            minus_s = keep.tile([P, V], F32, name=f"minus_s{t}")
+            plus_s = keep.tile([P, V], F32, name=f"plus_s{t}")
+            nc.scalar.activation(minus_s[:], s_banks[t][:], ACT.Copy, scale=-0.0625)
+            if t > 0:
+                nc.scalar.activation(plus_s[:], s_banks[t][:], ACT.Copy, scale=0.0625)
+            for u in range(2):
+                cols = slice(256 * u, 256 * (u + 1))
+                if t == 0:
+                    nc.scalar.activation(plus_s[:, cols], s_banks[t][:, cols], ACT.Copy, scale=0.0625)
+                result = keep.tile([P, 256], F32, name=f"result{t}{u}")
+                nc.vector.tensor_tensor(
+                    result[:], minus_s[:].indirect(n2_sb[:, 16 * u : 16 * (u + 1)]), plus_s[:, cols], ALU.add
+                )
+                nc.sync.dma_start(out_rows[:, t, cols], result[:])

@@ -1,6 +1,7 @@
 from contextlib import ExitStack
 
 import concourse.mybir as mybir
+from concourse.masks import make_identity
 
 K, T, S, V, G, H, C = 512, 2048, 1024, 512, 2048, 512, 512
 FLOPS = 2 * K * H * S + 2 * K * C * V
@@ -19,6 +20,7 @@ P = 128
 PACK = 4
 LANES = 16
 BANK = 512
+FIRST = 256
 CHUNKS = ((0, 256), (256, 128), (384, 128))
 
 
@@ -29,7 +31,6 @@ def tile_picked_pqcprmsdif_none_p_kernel(
     with ExitStack() as ctx:
         lists = ctx.enter_context(tc.tile_pool(name="lists", bufs=1))
         keep = ctx.enter_context(tc.tile_pool(name="keep", bufs=1))
-        ring = ctx.enter_context(tc.tile_pool(name="ring", bufs=2))
         psum = ctx.enter_context(tc.psum_pool(name="psum", bufs=1))
 
         k1_sb = lists.tile([P, H // LANES], U16, name="k1_sb")
@@ -51,20 +52,22 @@ def tile_picked_pqcprmsdif_none_p_kernel(
 
         d_words_rows = d_words[0].rearrange("p c r -> p (c r)").bitcast(I32)
         nc.sync.dma_start(k1_sb[:], k1)
-        nc.sync.dma_start(d_word_table[:, 0:BANK].bitcast(I32), d_words_rows[:, 0:BANK])
+        nc.sync.dma_start(d_word_table[:, 0:FIRST].bitcast(I32), d_words_rows[:, 0:FIRST])
         nc.sync.dma_start(d_byte_table[0:P:8, :].bitcast(I32), d_scales[0].bitcast(I32))
         nc.sync.dma_start(offs_sb[:], offs)
         for q in range(4):
             nc.sync.dma_start(
                 x_byte_table[32 * q : 32 * q + 4, :].bitcast(I32), x_scales[0, 4 * q : 4 * q + 4, :].bitcast(I32)
             )
-        nc.sync.dma_start(d_word_table[:, BANK:G].bitcast(I32), d_words_rows[:, BANK:G])
+        nc.sync.dma_start(d_word_table[:, FIRST:G].bitcast(I32), d_words_rows[:, FIRST:G])
         nc.sync.dma_start(x_word_table[:].bitcast(I32), x_words[0].rearrange("p c r -> p (c r)").bitcast(I32))
         nc.sync.dma_start(n1_sb[:], n1)
         nc.sync.dma_start(n2_sb[:], n2)
         nc.sync.dma_start(cand_sb[:], cand)
         nc.gpsimd.dma_start(gs_sb[:], gs.rearrange("(p t) o -> p (t o)", t=PACK))
 
+        ident = keep.tile([P, P], F32, name="ident")
+        make_identity(nc, ident[:])
         warm = keep.tile([P, 1], F32, name="warm")
         warm_in = keep.tile([P, 1], F32, name="warm_in")
         nc.gpsimd.memset(warm_in[:], 1.0)
@@ -112,69 +115,109 @@ def tile_picked_pqcprmsdif_none_p_kernel(
         nc.vector.tensor_copy(cand_bytes[:], x_byte_table[:].indirect(cand_sb[:]))
         cand_plane = keep.tile([P, PACK, P], U8, name="cand_plane", align_bytes=64)
         nc.vector.tensor_copy(cand_plane[:], cand_bytes[:].rearrange("p (m t) -> p t m", t=PACK))
-        s_banks = [psum.tile([P, V], F32, name=f"s_bank{t}", tag=f"bank{t}") for t in range(PACK)]
-        quantised = []
-        for n, (v0, width) in enumerate(CHUNKS):
-            planes = keep.tile([P, PACK, width], BF16, name=f"planes{n}", align_bytes=64)
-            for t in range(PACK):
-                lined = ring.tile([P, width, 2], F32, name=f"lined{n}{t}", tag="lined", align_bytes=64)
-                nc.vector.tensor_copy(
-                    lined[:].rearrange("p v e -> p (v e)"),
-                    sq[t][:].indirect(n1_sb[:, 2 * v0 // LANES : 2 * (v0 + width) // LANES]),
-                )
-                ms = ring.tile([P, width], F32, name=f"ms{n}{t}", tag="ms", bufs=3)
-                nc.vector.tensor_tensor(ms[:], lined[:, :, 0], lined[:, :, 1], ALU.add)
-                root = keep.tile([P, width], F32, name=f"root{n}{t}")
-                nc.scalar.activation(root[:], ms[:], ACT.Sqrt, bias=0.1)
-                nc.scalar.activation(planes[:, t, :], root[:], ACT.Copy, scale=gs_sb[:, t : t + 1])
-            if n == len(CHUNKS) - 1:
-                cand_picked = ring.tile([P, C], U32, name="cand_picked", tag="lined", align_bytes=64)
-                nc.vector.tensor_copy(cand_picked[:], x_word_table[:].indirect(cand_sb[:]))
-                cand_codes = keep.tile([P, PACK, P], U32, name="cand_codes", align_bytes=64)
-                nc.vector.tensor_copy(
-                    cand_codes[:].bitcast(I32), cand_picked[:].bitcast(I32).rearrange("p (m t) -> p t m", t=PACK)
-                )
-            z = keep.tile([P, width, PACK], BF16, name=f"z{n}", align_bytes=64)
-            nc.scalar.copy(
-                z[:].rearrange("p (c i) t -> p c t i", i=4), planes[:].rearrange("p t (c i) -> p c t i", i=4)
-            )
-            z_codes = keep.tile([P, width], U32, name=f"z_codes{n}", align_bytes=64)
-            z_plane = keep.tile([P, width], U8, name=f"z_plane{n}", align_bytes=64)
-            nc.vector.quantize_mx(
-                out=z_codes[:].bitcast(FP8X4), scales=z_plane[:], in_=z[:].rearrange("p v t -> p (v t)")
-            )
-            quantised.append((z_codes, z_plane))
+        z_codes = keep.tile([P, V], U32, name="z_codes", align_bytes=64)
+        z_plane = keep.tile([P, V], U8, name="z_plane", align_bytes=64)
 
-        def second_product(t, n):
-            v0, width = CHUNKS[n]
-            z_codes, z_plane = quantised[n]
+        def line_up(t, v0, width):
+            lined = keep.tile([P, width, 2], F32, name=f"lined{t}_{v0}", tag=f"lined{t}_{v0}", align_bytes=64)
+            nc.vector.tensor_copy(
+                lined[:].rearrange("p v e -> p (v e)"),
+                sq[t][:].indirect(n1_sb[:, 2 * v0 // LANES : 2 * (v0 + width) // LANES]),
+            )
+            return lined
+
+        def add_pairs_turned(dest, lined, b):
+            for e in range(2):
+                nc.tensor.matmul(
+                    dest, lined[:, b * P : (b + 1) * P, e], ident[:], start=e == 0, stop=e == 1, is_transpose=True
+                )
+
+        def quantise(z, v0, width):
+            nc.vector.quantize_mx(
+                out=z_codes[:, v0 : v0 + width].bitcast(FP8X4),
+                scales=z_plane[:, v0 : v0 + width],
+                in_=z[:].rearrange("p v u -> p (v u)").bitcast(BF16),
+            )
+
+        pairs = [keep.tile([P, 2, width], F32, name=f"pairs{n}") for n, (v0, width) in enumerate(CHUNKS)]
+
+        def weigh(t, pieces, chunk_ids, first_bank):
+            span = sum(CHUNKS[n][1] for n in chunk_ids)
+            start = CHUNKS[chunk_ids[0]][0]
+            blocks = span // P
+            sums = psum.tile([P, blocks, P], F32, name=f"sums{t}_{start}", tag=f"bank{first_bank}")
+            for v0, width in pieces:
+                lined = line_up(t, v0, width)
+                for b in range(width // P):
+                    add_pairs_turned(sums[:, (v0 - start) // P + b, :], lined, b)
+            roots = keep.tile([P, blocks, P], F32, name=f"roots{t}_{start}")
+            nc.scalar.activation(roots[:], sums[:], ACT.Sqrt, bias=0.1)
+            back = psum.tile([P, span], F32, name=f"back{t}_{start}", tag=f"bank{first_bank + 1}")
+            for b in range(blocks):
+                nc.tensor.transpose(back[:, b * P : (b + 1) * P], roots[:, b, :], ident[:])
+            for n in chunk_ids:
+                v0, width = CHUNKS[n]
+                halves = pairs[n][:, t // 2, :].bitcast(BF16).rearrange("p (v e) -> p v e", e=2)
+                nc.scalar.activation(
+                    halves[:, :, t % 2], back[:, v0 - start : v0 - start + width], ACT.Copy, scale=gs_sb[:, t : t + 1]
+                )
+
+        steps = [(t, ids) for t in range(PACK - 1) for ids in ((0,), (1, 2))]
+        steps += [(PACK - 1, (n,)) for n in range(len(CHUNKS))]
+        for j, (t, ids) in enumerate(steps):
+            weigh(t, ((CHUNKS[ids[0]][0], sum(CHUNKS[n][1] for n in ids)),), ids, 2 * j % 8)
+
+        cand_picked = keep.tile([P, C], U32, name="cand_picked", tag="lined3_0", align_bytes=64)
+        nc.vector.tensor_copy(cand_picked[:], x_word_table[:].indirect(cand_sb[:]))
+        cand_codes = keep.tile([P, PACK, P], U32, name="cand_codes", align_bytes=64)
+        nc.vector.tensor_copy(
+            cand_codes[:].bitcast(I32), cand_picked[:].bitcast(I32).rearrange("p (m t) -> p t m", t=PACK)
+        )
+
+        for n, (v0, width) in enumerate(CHUNKS):
+            z = keep.tile([P, width, 2], F32, name=f"z{n}", align_bytes=64)
+            nc.vector.tensor_copy(z[:], pairs[n][:].rearrange("p u v -> p v u"))
+            quantise(z, v0, width)
+
+        def second_product(dest, t, v0, width):
             nc.tensor.matmul_mx(
-                out=s_banks[t][:, v0 : v0 + width],
+                out=dest,
                 lhsT=cand_codes[:, t, :].bitcast(FP8X4),
                 lhsT_scale=cand_plane[:, t, :],
-                rhs=z_codes[:].bitcast(FP8X4),
-                rhs_scale=z_plane[:],
+                rhs=z_codes[:, v0 : v0 + width].bitcast(FP8X4),
+                rhs_scale=z_plane[:, v0 : v0 + width],
                 start=True,
                 stop=True,
             )
 
-        for t in range(PACK):
-            for n in range(len(CHUNKS)):
-                second_product(t, n)
-
         out_rows = out.rearrange("(p t) v -> p t v", t=PACK)
+        windows = [keep.tile([P, V if t == 0 else 2 * V], F32, name=f"window{t}") for t in range(PACK)]
+        last_plus = keep.tile([P, V], F32, name="last_plus")
         for t in range(PACK):
-            minus_s = keep.tile([P, V], F32, name=f"minus_s{t}")
-            plus_s = keep.tile([P, V], F32, name=f"plus_s{t}")
-            nc.scalar.activation(minus_s[:], s_banks[t][:], ACT.Copy, scale=-0.0625)
-            if t > 0:
-                nc.scalar.activation(plus_s[:], s_banks[t][:], ACT.Copy, scale=0.0625)
-            for u in range(2):
-                cols = slice(256 * u, 256 * (u + 1))
-                if t == 0:
-                    nc.scalar.activation(plus_s[:, cols], s_banks[t][:, cols], ACT.Copy, scale=0.0625)
-                result = keep.tile([P, 256], F32, name=f"result{t}{u}")
+            minus_s = windows[t][:, 0:V]
+            plus_s = windows[t + 1][:, V : 2 * V] if t + 1 < PACK else last_plus[:]
+            if t == 0:
+                early = psum.tile([P, 384], F32, name="s_early", tag="bank2")
+                late = psum.tile([P, 128], F32, name="s_late", tag="bank3")
+                for v0, width in CHUNKS[:2]:
+                    second_product(early[:, v0 : v0 + width], t, v0, width)
+                second_product(late[:], t, 384, 128)
+                parts = ((early, slice(0, 384)), (late, slice(384, 512)))
+            else:
+                whole = psum.tile([P, V], F32, name=f"s_bank{t}", tag=f"bank{3 + t}")
+                second_product(whole[:], t, 0, V)
+                parts = ((whole, slice(0, V)),)
+            for bank, cols in parts:
+                nc.scalar.activation(minus_s[:, cols], bank[:], ACT.Copy, scale=-0.0625)
+                nc.scalar.activation(plus_s[:, cols], bank[:], ACT.Copy, scale=0.0625)
+            piece = 256 if t in (0, PACK - 1) else V
+            for c0 in range(0, V, piece):
+                cols = slice(c0, c0 + piece)
+                result = keep.tile([P, piece], F32, name=f"result{t}_{c0}")
                 nc.vector.tensor_tensor(
-                    result[:], minus_s[:].indirect(n2_sb[:, 16 * u : 16 * (u + 1)]), plus_s[:, cols], ALU.add
+                    result[:],
+                    windows[t][:].indirect(n2_sb[:, c0 // LANES : (c0 + piece) // LANES]),
+                    plus_s[:, cols],
+                    ALU.add,
                 )
                 nc.sync.dma_start(out_rows[:, t, cols], result[:])

@@ -20,7 +20,6 @@ P = 128
 PACK = 4
 LANES = 16
 BANK = 512
-FIRST = 256
 CHUNKS = ((0, 256), (256, 128), (384, 128))
 
 
@@ -46,25 +45,23 @@ def tile_picked_pqcprmsdif_none_p_kernel(
         d_plane = keep.tile([P, H], U8, name="d_plane", align_bytes=64)
         gs_sb = keep.tile([P, PACK], F32, name="gs_sb")
 
-        nc.gpsimd.memset(d_byte_table[:].bitcast(I32), 0)
+        nc.vector.memset(d_byte_table[:].bitcast(I32), 0)
         nc.vector.memset(x_byte_table[:].bitcast(I32), 0)
         nc.gpsimd.memset(d_plane[:].bitcast(I32), 0)
 
-        d_words_rows = d_words[0].rearrange("p c r -> p (c r)").bitcast(I32)
         nc.sync.dma_start(k1_sb[:], k1)
-        nc.sync.dma_start(d_word_table[:, 0:FIRST].bitcast(I32), d_words_rows[:, 0:FIRST])
         nc.sync.dma_start(d_byte_table[0:P:8, :].bitcast(I32), d_scales[0].bitcast(I32))
         nc.sync.dma_start(offs_sb[:], offs)
         for q in range(4):
             nc.sync.dma_start(
                 x_byte_table[32 * q : 32 * q + 4, :].bitcast(I32), x_scales[0, 4 * q : 4 * q + 4, :].bitcast(I32)
             )
-        nc.sync.dma_start(d_word_table[:, FIRST:G].bitcast(I32), d_words_rows[:, FIRST:G])
+        nc.sync.dma_start(d_word_table[:].bitcast(I32), d_words[0].rearrange("p c r -> p (c r)").bitcast(I32))
         nc.sync.dma_start(x_word_table[:].bitcast(I32), x_words[0].rearrange("p c r -> p (c r)").bitcast(I32))
         nc.sync.dma_start(n1_sb[:], n1)
         nc.sync.dma_start(n2_sb[:], n2)
         nc.sync.dma_start(cand_sb[:], cand)
-        nc.gpsimd.dma_start(gs_sb[:], gs.rearrange("(p t) o -> p (t o)", t=PACK))
+        nc.sync.dma_start(gs_sb[:], gs.rearrange("(p t) o -> p (t o)", t=PACK))
 
         ident = keep.tile([P, P], F32, name="ident")
         make_identity(nc, ident[:])
@@ -73,10 +70,15 @@ def tile_picked_pqcprmsdif_none_p_kernel(
         nc.gpsimd.memset(warm_in[:], 1.0)
         nc.scalar.activation(warm[:], warm_in[:], ACT.Sqrt)
 
+        def deal(dest, src, run):
+            nc.vector.tensor_copy(
+                dest.rearrange("p t (c i) -> p c t i", i=run), src.rearrange("p (c i t) -> p c t i", i=run, t=PACK)
+            )
+
         d_bytes = keep.tile([P, H], U8, name="d_bytes", align_bytes=64)
         nc.vector.tensor_copy(d_bytes[:], d_byte_table[:].indirect(k1_sb[:]))
         d_bytes_dealt = keep.tile([P, PACK, P], U8, name="d_bytes_dealt", align_bytes=64)
-        nc.vector.tensor_copy(d_bytes_dealt[:], d_bytes[:].rearrange("p (m t) -> p t m", t=PACK))
+        deal(d_bytes_dealt[:], d_bytes[:], 16)
         dealt_rows = d_bytes_dealt[:].rearrange("p t m -> p (t m)")
         for c in range(4):
             nc.scalar.dma_start(d_plane[c:P:32, :].bitcast(I32), dealt_rows[8 * c : P : 32, :].bitcast(I32))
@@ -87,7 +89,7 @@ def tile_picked_pqcprmsdif_none_p_kernel(
         d_picked = keep.tile([P, H], U32, name="d_picked", align_bytes=64)
         nc.vector.tensor_copy(d_picked[:], d_word_table[:].indirect(k1_sb[:]))
         d_codes = keep.tile([P, PACK, P], U32, name="d_codes", align_bytes=64)
-        nc.vector.tensor_copy(d_codes[:].bitcast(I32), d_picked[:].bitcast(I32).rearrange("p (m t) -> p t m", t=PACK))
+        deal(d_codes[:].bitcast(I32), d_picked[:].bitcast(I32), 4)
 
         xq_words = [keep.tile([P, BANK], U32, name=f"xq_words{u}", align_bytes=64) for u in range(2)]
         for u in range(2):
@@ -114,7 +116,7 @@ def tile_picked_pqcprmsdif_none_p_kernel(
         cand_bytes = keep.tile([P, C], U8, name="cand_bytes", align_bytes=64)
         nc.vector.tensor_copy(cand_bytes[:], x_byte_table[:].indirect(cand_sb[:]))
         cand_plane = keep.tile([P, PACK, P], U8, name="cand_plane", align_bytes=64)
-        nc.vector.tensor_copy(cand_plane[:], cand_bytes[:].rearrange("p (m t) -> p t m", t=PACK))
+        deal(cand_plane[:], cand_bytes[:], 16)
         z_codes = keep.tile([P, V], U32, name="z_codes", align_bytes=64)
         z_plane = keep.tile([P, V], U8, name="z_plane", align_bytes=64)
 
@@ -165,14 +167,13 @@ def tile_picked_pqcprmsdif_none_p_kernel(
         steps = [(t, ids) for t in range(PACK - 1) for ids in ((0,), (1, 2))]
         steps += [(PACK - 1, (n,)) for n in range(len(CHUNKS))]
         for j, (t, ids) in enumerate(steps):
-            weigh(t, ((CHUNKS[ids[0]][0], sum(CHUNKS[n][1] for n in ids)),), ids, 2 * j % 8)
+            lo, hi = CHUNKS[ids[0]][0], sum(CHUNKS[ids[-1]])
+            weigh(t, [(v0, min(256, hi - v0)) for v0 in range(lo, hi, 256)], ids, 2 * j % 8)
 
         cand_picked = keep.tile([P, C], U32, name="cand_picked", tag="lined3_0", align_bytes=64)
         nc.vector.tensor_copy(cand_picked[:], x_word_table[:].indirect(cand_sb[:]))
         cand_codes = keep.tile([P, PACK, P], U32, name="cand_codes", align_bytes=64)
-        nc.vector.tensor_copy(
-            cand_codes[:].bitcast(I32), cand_picked[:].bitcast(I32).rearrange("p (m t) -> p t m", t=PACK)
-        )
+        deal(cand_codes[:].bitcast(I32), cand_picked[:].bitcast(I32), 4)
 
         for n, (v0, width) in enumerate(CHUNKS):
             z = keep.tile([P, width, 2], F32, name=f"z{n}", align_bytes=64)

@@ -19,7 +19,10 @@ ALU = mybir.AluOpType
 P = 128
 PACK = 4
 LANES = 16
+QUADRANT = 32
 BANK = 512
+BANKS = 8
+SIXTEENTH = 0.0625
 CHUNKS = ((0, 256), (256, 128), (384, 128))
 
 
@@ -52,23 +55,16 @@ def tile_picked_pqcprmsdif_none_p_kernel(
         nc.sync.dma_start(k1_sb[:], k1)
         nc.sync.dma_start(d_byte_table[0:P:8, :].bitcast(I32), d_scales[0].bitcast(I32))
         nc.sync.dma_start(offs_sb[:], offs)
-        for q in range(4):
+        for q in range(P // QUADRANT):
             nc.sync.dma_start(
-                x_byte_table[32 * q : 32 * q + 4, :].bitcast(I32), x_scales[0, 4 * q : 4 * q + 4, :].bitcast(I32)
+                x_byte_table[QUADRANT * q : QUADRANT * q + 4, :].bitcast(I32),
+                x_scales[0, 4 * q : 4 * q + 4, :].bitcast(I32),
             )
         nc.sync.dma_start(d_word_table[:].bitcast(I32), d_words[0].rearrange("p c r -> p (c r)").bitcast(I32))
         nc.sync.dma_start(x_word_table[:].bitcast(I32), x_words[0].rearrange("p c r -> p (c r)").bitcast(I32))
-        nc.sync.dma_start(n1_sb[:], n1)
-        nc.sync.dma_start(n2_sb[:], n2)
-        nc.sync.dma_start(cand_sb[:], cand)
-        nc.sync.dma_start(gs_sb[:], gs.rearrange("(p t) o -> p (t o)", t=PACK))
 
         ident = keep.tile([P, P], F32, name="ident")
         make_identity(nc, ident[:])
-        warm = keep.tile([P, 1], F32, name="warm")
-        warm_in = keep.tile([P, 1], F32, name="warm_in")
-        nc.gpsimd.memset(warm_in[:], 1.0)
-        nc.scalar.activation(warm[:], warm_in[:], ACT.Sqrt)
 
         def deal(dest, src, run):
             nc.vector.tensor_copy(
@@ -81,7 +77,12 @@ def tile_picked_pqcprmsdif_none_p_kernel(
         deal(d_bytes_dealt[:], d_bytes[:], 16)
         dealt_rows = d_bytes_dealt[:].rearrange("p t m -> p (t m)")
         for c in range(4):
-            nc.scalar.dma_start(d_plane[c:P:32, :].bitcast(I32), dealt_rows[8 * c : P : 32, :].bitcast(I32))
+            nc.sync.dma_start(d_plane[c:P:QUADRANT, :].bitcast(I32), dealt_rows[8 * c : P : QUADRANT, :].bitcast(I32))
+
+        nc.sync.dma_start(cand_sb[:], cand)
+        nc.sync.dma_start(n1_sb[:], n1)
+        nc.sync.dma_start(gs_sb[:], gs.rearrange("(p t) o -> p (t o)", t=PACK))
+        nc.sync.dma_start(n2_sb[:], n2)
 
         xq_bytes = keep.tile([P, S], U8, name="xq_bytes", align_bytes=64)
         nc.vector.tensor_copy(xq_bytes[:], x_byte_table[:].indirect(offs_sb[:]))
@@ -93,7 +94,8 @@ def tile_picked_pqcprmsdif_none_p_kernel(
 
         xq_words = [keep.tile([P, BANK], U32, name=f"xq_words{u}", align_bytes=64) for u in range(2)]
         for u in range(2):
-            nc.vector.tensor_copy(xq_words[u][:], x_word_table[:].indirect(offs_sb[:, 32 * u : 32 * (u + 1)]))
+            entries = offs_sb[:, u * BANK // LANES : (u + 1) * BANK // LANES]
+            nc.vector.tensor_copy(xq_words[u][:], x_word_table[:].indirect(entries))
 
         sq = [keep.tile([P, S], F32, name=f"sq{t}") for t in range(PACK)]
 
@@ -108,50 +110,44 @@ def tile_picked_pqcprmsdif_none_p_kernel(
                 start=True,
                 stop=True,
             )
-            nc.scalar.activation(sq[t][:, u * BANK : (u + 1) * BANK], bank[:], ACT.Square, scale=0.0625)
+            nc.scalar.activation(sq[t][:, u * BANK : (u + 1) * BANK], bank[:], ACT.Square, scale=SIXTEENTH)
 
-        for t, u in ((0, 0), (1, 0), (0, 1), (1, 1), (2, 0), (2, 1), (3, 0), (3, 1)):
-            first_product(t, u)
+        for u in range(2):
+            for t in range(2):
+                first_product(t, u)
+        for t in range(2, PACK):
+            for u in range(2):
+                first_product(t, u)
 
         cand_bytes = keep.tile([P, C], U8, name="cand_bytes", align_bytes=64)
         nc.vector.tensor_copy(cand_bytes[:], x_byte_table[:].indirect(cand_sb[:]))
         cand_plane = keep.tile([P, PACK, P], U8, name="cand_plane", align_bytes=64)
         deal(cand_plane[:], cand_bytes[:], 16)
+
         z_codes = keep.tile([P, V], U32, name="z_codes", align_bytes=64)
         z_plane = keep.tile([P, V], U8, name="z_plane", align_bytes=64)
-
-        def line_up(t, v0, width):
-            lined = keep.tile([P, width, 2], F32, name=f"lined{t}_{v0}", tag=f"lined{t}_{v0}", align_bytes=64)
-            nc.vector.tensor_copy(
-                lined[:].rearrange("p v e -> p (v e)"),
-                sq[t][:].indirect(n1_sb[:, 2 * v0 // LANES : 2 * (v0 + width) // LANES]),
-            )
-            return lined
-
-        def add_pairs_turned(dest, lined, b):
-            for e in range(2):
-                nc.tensor.matmul(
-                    dest, lined[:, b * P : (b + 1) * P, e], ident[:], start=e == 0, stop=e == 1, is_transpose=True
-                )
-
-        def quantise(z, v0, width):
-            nc.vector.quantize_mx(
-                out=z_codes[:, v0 : v0 + width].bitcast(FP8X4),
-                scales=z_plane[:, v0 : v0 + width],
-                in_=z[:].rearrange("p v u -> p (v u)").bitcast(BF16),
-            )
-
         pairs = [keep.tile([P, 2, width], F32, name=f"pairs{n}") for n, (v0, width) in enumerate(CHUNKS)]
 
-        def weigh(t, pieces, chunk_ids, first_bank):
-            span = sum(CHUNKS[n][1] for n in chunk_ids)
+        def weigh(t, chunk_ids, first_bank):
             start = CHUNKS[chunk_ids[0]][0]
+            span = sum(CHUNKS[n][1] for n in chunk_ids)
             blocks = span // P
             sums = psum.tile([P, blocks, P], F32, name=f"sums{t}_{start}", tag=f"bank{first_bank}")
-            for v0, width in pieces:
-                lined = line_up(t, v0, width)
-                for b in range(width // P):
-                    add_pairs_turned(sums[:, (v0 - start) // P + b, :], lined, b)
+            lined = keep.tile([P, span, 2], F32, name=f"lined{t}_{start}", tag=f"lined{t}_{start}", align_bytes=64)
+            nc.vector.tensor_copy(
+                lined[:].rearrange("p v e -> p (v e)"),
+                sq[t][:].indirect(n1_sb[:, 2 * start // LANES : 2 * (start + span) // LANES]),
+            )
+            for b in range(blocks):
+                for e in range(2):
+                    nc.tensor.matmul(
+                        sums[:, b, :],
+                        lined[:, b * P : (b + 1) * P, e],
+                        ident[:],
+                        start=e == 0,
+                        stop=e == 1,
+                        is_transpose=True,
+                    )
             roots = keep.tile([P, blocks, P], F32, name=f"roots{t}_{start}")
             nc.scalar.activation(roots[:], sums[:], ACT.Sqrt, bias=0.1)
             back = psum.tile([P, span], F32, name=f"back{t}_{start}", tag=f"bank{first_bank + 1}")
@@ -167,10 +163,9 @@ def tile_picked_pqcprmsdif_none_p_kernel(
         steps = [(t, ids) for t in range(PACK - 1) for ids in ((0,), (1, 2))]
         steps += [(PACK - 1, (n,)) for n in range(len(CHUNKS))]
         for j, (t, ids) in enumerate(steps):
-            lo, hi = CHUNKS[ids[0]][0], sum(CHUNKS[ids[-1]])
-            weigh(t, [(v0, min(256, hi - v0)) for v0 in range(lo, hi, 256)], ids, 2 * j % 8)
+            weigh(t, ids, 2 * j % BANKS)
 
-        cand_picked = keep.tile([P, C], U32, name="cand_picked", tag="lined3_0", align_bytes=64)
+        cand_picked = keep.tile([P, C], U32, name="cand_picked", tag=f"lined{PACK - 1}_0", align_bytes=64)
         nc.vector.tensor_copy(cand_picked[:], x_word_table[:].indirect(cand_sb[:]))
         cand_codes = keep.tile([P, PACK, P], U32, name="cand_codes", align_bytes=64)
         deal(cand_codes[:].bitcast(I32), cand_picked[:].bitcast(I32), 4)
@@ -178,7 +173,11 @@ def tile_picked_pqcprmsdif_none_p_kernel(
         for n, (v0, width) in enumerate(CHUNKS):
             z = keep.tile([P, width, 2], F32, name=f"z{n}", align_bytes=64)
             nc.vector.tensor_copy(z[:], pairs[n][:].rearrange("p u v -> p v u"))
-            quantise(z, v0, width)
+            nc.vector.quantize_mx(
+                out=z_codes[:, v0 : v0 + width].bitcast(FP8X4),
+                scales=z_plane[:, v0 : v0 + width],
+                in_=z[:].rearrange("p v u -> p (v u)").bitcast(BF16),
+            )
 
         def second_product(dest, t, v0, width):
             nc.tensor.matmul_mx(
@@ -194,24 +193,26 @@ def tile_picked_pqcprmsdif_none_p_kernel(
         out_rows = out.rearrange("(p t) v -> p t v", t=PACK)
         windows = [keep.tile([P, V if t == 0 else 2 * V], F32, name=f"window{t}") for t in range(PACK)]
         last_plus = keep.tile([P, V], F32, name="last_plus")
+        first_free = 2 * len(steps) % BANKS
+        last_start, last_width = CHUNKS[-1]
         for t in range(PACK):
             minus_s = windows[t][:, 0:V]
             plus_s = windows[t + 1][:, V : 2 * V] if t + 1 < PACK else last_plus[:]
             if t == 0:
-                early = psum.tile([P, 384], F32, name="s_early", tag="bank2")
-                late = psum.tile([P, 128], F32, name="s_late", tag="bank3")
-                for v0, width in CHUNKS[:2]:
+                early = psum.tile([P, last_start], F32, name="s_early", tag=f"bank{first_free}")
+                late = psum.tile([P, last_width], F32, name="s_late", tag=f"bank{first_free + 1}")
+                for v0, width in CHUNKS[:-1]:
                     second_product(early[:, v0 : v0 + width], t, v0, width)
-                second_product(late[:], t, 384, 128)
-                parts = ((early, slice(0, 384)), (late, slice(384, 512)))
+                second_product(late[:], t, last_start, last_width)
+                parts = ((early, slice(0, last_start)), (late, slice(last_start, V)))
             else:
-                whole = psum.tile([P, V], F32, name=f"s_bank{t}", tag=f"bank{3 + t}")
+                whole = psum.tile([P, V], F32, name=f"s_bank{t}", tag=f"bank{first_free + 1 + t}")
                 second_product(whole[:], t, 0, V)
                 parts = ((whole, slice(0, V)),)
             for bank, cols in parts:
-                nc.scalar.activation(minus_s[:, cols], bank[:], ACT.Copy, scale=-0.0625)
-                nc.scalar.activation(plus_s[:, cols], bank[:], ACT.Copy, scale=0.0625)
-            piece = 256 if t in (0, PACK - 1) else V
+                nc.scalar.activation(minus_s[:, cols], bank[:], ACT.Copy, scale=-SIXTEENTH)
+                nc.scalar.activation(plus_s[:, cols], bank[:], ACT.Copy, scale=SIXTEENTH)
+            piece = V // 2 if t in (0, PACK - 1) else V
             for c0 in range(0, V, piece):
                 cols = slice(c0, c0 + piece)
                 result = keep.tile([P, piece], F32, name=f"result{t}_{c0}")

from contextlib import ExitStack

import concourse.mybir as mybir
from concourse.masks import make_identity

K, T, S, V, G, H, C = 512, 2048, 1024, 512, 2048, 512, 512
FLOPS = 2 * K * H * S + 2 * K * C * V

F32 = mybir.dt.float32
BF16 = mybir.dt.bfloat16
I32 = mybir.dt.int32
U32 = mybir.dt.uint32
U16 = mybir.dt.uint16
U8 = mybir.dt.uint8
FP8X4 = mybir.dt.float8_e4m3fn_x4
ACT = mybir.ActivationFunctionType
ALU = mybir.AluOpType

P = 128
PACK = 4
LANES = 16
QUADRANT = 32
BANK = 512
BANKS = 8
SIXTEENTH = 0.0625
CHUNKS = ((0, 256), (256, 128), (384, 128))


def tile_picked_pqcprmsdif_none_p_kernel(
    tc, x_words, x_scales, d_words, d_scales, gs, offs, k1, n1, cand, n2, out
):
    nc = tc.nc
    with ExitStack() as ctx:
        lists = ctx.enter_context(tc.tile_pool(name="lists", bufs=1))
        keep = ctx.enter_context(tc.tile_pool(name="keep", bufs=1))
        psum = ctx.enter_context(tc.psum_pool(name="psum", bufs=1))

        k1_sb = lists.tile([P, H // LANES], U16, name="k1_sb")
        offs_sb = lists.tile([P, S // LANES], U16, name="offs_sb")
        cand_sb = lists.tile([P, C // LANES], U16, name="cand_sb")
        n1_sb = lists.tile([P, S // LANES], U16, name="n1_sb")
        n2_sb = lists.tile([P, V // LANES], U16, name="n2_sb")

        d_byte_table = keep.tile([P, G], U8, name="d_byte_table", align_bytes=64)
        x_byte_table = keep.tile([P, T], U8, name="x_byte_table", align_bytes=64)
        d_word_table = keep.tile([P, G], U32, name="d_word_table", align_bytes=64)
        x_word_table = keep.tile([P, T], U32, name="x_word_table", align_bytes=64)
        d_plane = keep.tile([P, H], U8, name="d_plane", align_bytes=64)
        gs_sb = keep.tile([P, PACK], F32, name="gs_sb")

        nc.vector.memset(d_byte_table[:].bitcast(I32), 0)
        nc.vector.memset(x_byte_table[:].bitcast(I32), 0)
        nc.gpsimd.memset(d_plane[:].bitcast(I32), 0)

        nc.sync.dma_start(k1_sb[:], k1)
        nc.sync.dma_start(d_byte_table[0:P:8, :].bitcast(I32), d_scales[0].bitcast(I32))
        nc.sync.dma_start(offs_sb[:], offs)
        for q in range(P // QUADRANT):
            nc.sync.dma_start(
                x_byte_table[QUADRANT * q : QUADRANT * q + 4, :].bitcast(I32),
                x_scales[0, 4 * q : 4 * q + 4, :].bitcast(I32),
            )
        nc.sync.dma_start(d_word_table[:].bitcast(I32), d_words[0].rearrange("p c r -> p (c r)").bitcast(I32))
        nc.sync.dma_start(x_word_table[:].bitcast(I32), x_words[0].rearrange("p c r -> p (c r)").bitcast(I32))

        ident = keep.tile([P, P], F32, name="ident")
        make_identity(nc, ident[:])

        def deal(dest, src, run):
            nc.vector.tensor_copy(
                dest.rearrange("p t (c i) -> p c t i", i=run), src.rearrange("p (c i t) -> p c t i", i=run, t=PACK)
            )

        d_bytes = keep.tile([P, H], U8, name="d_bytes", align_bytes=64)
        nc.vector.tensor_copy(d_bytes[:], d_byte_table[:].indirect(k1_sb[:]))
        d_bytes_dealt = keep.tile([P, PACK, P], U8, name="d_bytes_dealt", align_bytes=64)
        deal(d_bytes_dealt[:], d_bytes[:], 16)
        dealt_rows = d_bytes_dealt[:].rearrange("p t m -> p (t m)")
        for c in range(4):
            nc.sync.dma_start(d_plane[c:P:QUADRANT, :].bitcast(I32), dealt_rows[8 * c : P : QUADRANT, :].bitcast(I32))

        nc.sync.dma_start(cand_sb[:], cand)
        nc.sync.dma_start(n1_sb[:], n1)
        nc.sync.dma_start(gs_sb[:], gs.rearrange("(p t) o -> p (t o)", t=PACK))
        nc.sync.dma_start(n2_sb[:], n2)

        xq_bytes = keep.tile([P, S], U8, name="xq_bytes", align_bytes=64)
        nc.vector.tensor_copy(xq_bytes[:], x_byte_table[:].indirect(offs_sb[:]))

        d_picked = keep.tile([P, H], U32, name="d_picked", align_bytes=64)
        nc.vector.tensor_copy(d_picked[:], d_word_table[:].indirect(k1_sb[:]))
        d_codes = keep.tile([P, PACK, P], U32, name="d_codes", align_bytes=64)
        deal(d_codes[:].bitcast(I32), d_picked[:].bitcast(I32), 4)

        xq_words = [keep.tile([P, BANK], U32, name=f"xq_words{u}", align_bytes=64) for u in range(2)]
        for u in range(2):
            entries = offs_sb[:, u * BANK // LANES : (u + 1) * BANK // LANES]
            nc.vector.tensor_copy(xq_words[u][:], x_word_table[:].indirect(entries))

        sq = [keep.tile([P, S], F32, name=f"sq{t}") for t in range(PACK)]

        def first_product(t, u):
            bank = psum.tile([P, BANK], F32, name=f"h_bank{t}{u}", tag=f"bank{2 * t + u}")
            nc.tensor.matmul_mx(
                out=bank[:],
                lhsT=d_codes[:, t, :].bitcast(FP8X4),
                lhsT_scale=d_plane[:, t * P : (t + 1) * P],
                rhs=xq_words[u][:].bitcast(FP8X4),
                rhs_scale=xq_bytes[:, u * BANK : (u + 1) * BANK],
                start=True,
                stop=True,
            )
            nc.scalar.activation(sq[t][:, u * BANK : (u + 1) * BANK], bank[:], ACT.Square, scale=SIXTEENTH)

        for u in range(2):
            for t in range(2):
                first_product(t, u)
        for t in range(2, PACK):
            for u in range(2):
                first_product(t, u)

        cand_bytes = keep.tile([P, C], U8, name="cand_bytes", align_bytes=64)
        nc.vector.tensor_copy(cand_bytes[:], x_byte_table[:].indirect(cand_sb[:]))
        cand_plane = keep.tile([P, PACK, P], U8, name="cand_plane", align_bytes=64)
        deal(cand_plane[:], cand_bytes[:], 16)

        z_codes = keep.tile([P, V], U32, name="z_codes", align_bytes=64)
        z_plane = keep.tile([P, V], U8, name="z_plane", align_bytes=64)
        pairs = [keep.tile([P, 2, width], F32, name=f"pairs{n}") for n, (v0, width) in enumerate(CHUNKS)]

        def weigh(t, chunk_ids, first_bank):
            start = CHUNKS[chunk_ids[0]][0]
            span = sum(CHUNKS[n][1] for n in chunk_ids)
            blocks = span // P
            sums = psum.tile([P, blocks, P], F32, name=f"sums{t}_{start}", tag=f"bank{first_bank}")
            lined = keep.tile([P, span, 2], F32, name=f"lined{t}_{start}", tag=f"lined{t}_{start}", align_bytes=64)
            nc.vector.tensor_copy(
                lined[:].rearrange("p v e -> p (v e)"),
                sq[t][:].indirect(n1_sb[:, 2 * start // LANES : 2 * (start + span) // LANES]),
            )
            for b in range(blocks):
                for e in range(2):
                    nc.tensor.matmul(
                        sums[:, b, :],
                        lined[:, b * P : (b + 1) * P, e],
                        ident[:],
                        start=e == 0,
                        stop=e == 1,
                        is_transpose=True,
                    )
            roots = keep.tile([P, blocks, P], F32, name=f"roots{t}_{start}")
            nc.scalar.activation(roots[:], sums[:], ACT.Sqrt, bias=0.1)
            back = psum.tile([P, span], F32, name=f"back{t}_{start}", tag=f"bank{first_bank + 1}")
            for b in range(blocks):
                nc.tensor.transpose(back[:, b * P : (b + 1) * P], roots[:, b, :], ident[:])
            for n in chunk_ids:
                v0, width = CHUNKS[n]
                halves = pairs[n][:, t // 2, :].bitcast(BF16).rearrange("p (v e) -> p v e", e=2)
                nc.scalar.activation(
                    halves[:, :, t % 2], back[:, v0 - start : v0 - start + width], ACT.Copy, scale=gs_sb[:, t : t + 1]
                )

        steps = [(t, ids) for t in range(PACK - 1) for ids in ((0,), (1, 2))]
        steps += [(PACK - 1, (n,)) for n in range(len(CHUNKS))]
        for j, (t, ids) in enumerate(steps):
            weigh(t, ids, 2 * j % BANKS)

        cand_picked = keep.tile([P, C], U32, name="cand_picked", tag=f"lined{PACK - 1}_0", align_bytes=64)
        nc.vector.tensor_copy(cand_picked[:], x_word_table[:].indirect(cand_sb[:]))
        cand_codes = keep.tile([P, PACK, P], U32, name="cand_codes", align_bytes=64)
        deal(cand_codes[:].bitcast(I32), cand_picked[:].bitcast(I32), 4)

        for n, (v0, width) in enumerate(CHUNKS):
            z = keep.tile([P, width, 2], F32, name=f"z{n}", align_bytes=64)
            nc.vector.tensor_copy(z[:], pairs[n][:].rearrange("p u v -> p v u"))
            nc.vector.quantize_mx(
                out=z_codes[:, v0 : v0 + width].bitcast(FP8X4),
                scales=z_plane[:, v0 : v0 + width],
                in_=z[:].rearrange("p v u -> p (v u)").bitcast(BF16),
            )

        def second_product(dest, t, v0, width):
            nc.tensor.matmul_mx(
                out=dest,
                lhsT=cand_codes[:, t, :].bitcast(FP8X4),
                lhsT_scale=cand_plane[:, t, :],
                rhs=z_codes[:, v0 : v0 + width].bitcast(FP8X4),
                rhs_scale=z_plane[:, v0 : v0 + width],
                start=True,
                stop=True,
            )

        out_rows = out.rearrange("(p t) v -> p t v", t=PACK)
        windows = [keep.tile([P, V if t == 0 else 2 * V], F32, name=f"window{t}") for t in range(PACK)]
        last_plus = keep.tile([P, V], F32, name="last_plus")
        first_free = 2 * len(steps) % BANKS
        last_start, last_width = CHUNKS[-1]
        for t in range(PACK):
            minus_s = windows[t][:, 0:V]
            plus_s = windows[t + 1][:, V : 2 * V] if t + 1 < PACK else last_plus[:]
            if t == 0:
                early = psum.tile([P, last_start], F32, name="s_early", tag=f"bank{first_free}")
                late = psum.tile([P, last_width], F32, name="s_late", tag=f"bank{first_free + 1}")
                for v0, width in CHUNKS[:-1]:
                    second_product(early[:, v0 : v0 + width], t, v0, width)
                second_product(late[:], t, last_start, last_width)
                parts = ((early, slice(0, last_start)), (late, slice(last_start, V)))
            else:
                whole = psum.tile([P, V], F32, name=f"s_bank{t}", tag=f"bank{first_free + 1 + t}")
                second_product(whole[:], t, 0, V)
                parts = ((whole, slice(0, V)),)
            for bank, cols in parts:
                nc.scalar.activation(minus_s[:, cols], bank[:], ACT.Copy, scale=-SIXTEENTH)
                nc.scalar.activation(plus_s[:, cols], bank[:], ACT.Copy, scale=SIXTEENTH)
            piece = V // 2 if t in (0, PACK - 1) else V
            for c0 in range(0, V, piece):
                cols = slice(c0, c0 + piece)
                result = keep.tile([P, piece], F32, name=f"result{t}_{c0}")
                nc.vector.tensor_tensor(
                    result[:],
                    windows[t][:].indirect(n2_sb[:, c0 // LANES : (c0 + piece) // LANES]),
                    plus_s[:, cols],
                    ALU.add,
                )
                nc.sync.dma_start(out_rows[:, t, cols], result[:])
